import numpy as np
import ml_dtypes


def mxq(x, axis, fmt="e4m3"):
    dtype, down = {"e4m3": (ml_dtypes.float8_e4m3fn, 7), "e5m2": (ml_dtypes.float8_e5m2, 14)}[fmt]
    v = np.moveaxis(np.asarray(x, np.float32).astype(ml_dtypes.bfloat16).astype(np.float64), axis, -1)
    blocks = v.reshape(v.shape[:-1] + (-1, 32))
    amax = np.abs(blocks).max(-1, keepdims=True)
    byte = np.maximum(np.where(amax > 0, np.frexp(amax)[1] - 1 + 127, 0) - down, 1)
    scale = np.exp2(byte - 127.0)
    codes = (blocks / scale).astype(np.float32).astype(dtype).astype(np.float64)
    return np.moveaxis((codes * scale).reshape(v.shape), -1, axis)


WIDE = False


def mx_kscale(k):
    if not WIDE:
        return np.ones(k)
    levels = np.array([10, -10, 5, -5, 0])
    if k % 512:
        return np.exp2(np.random.permutation(np.resize(levels, k // 32))).repeat(32)
    a = np.empty((k // 512, 16))
    for p in range(k // 512):
        a[p, :8] = np.random.permutation(np.resize(levels, 8))
        for g in range(8):
            far = levels[np.abs(levels - a[p, g]) >= 10]
            a[p, g + 8] = far[np.random.randint(len(far))]
    return np.exp2(a.ravel()).repeat(32)


def f64(x):
    return np.asarray(x).astype(np.float64)


def striped(idx):
    return np.tile(idx.reshape(-1, 16).T, (8, 1)).astype(np.uint16)


def unstriped(offs):
    return offs[:16].T.reshape(-1).astype(np.int64)


def pack_weight(w):
    k, n = w.shape
    w = f64(np.asarray(w, np.float32).astype(ml_dtypes.bfloat16)).reshape(k // 32, 32, n)
    amax = np.abs(w).max(1)
    byte = np.clip(np.where(amax > 0, np.frexp(amax)[1] - 1 + 127 - 7, 1), 1, 254)
    scaled = (w * np.exp2(127.0 - byte)[:, None, :]).reshape(k, n).astype(np.float32)
    words = np.ascontiguousarray(scaled.reshape(k // 512, 128, 4, n).transpose(0, 1, 3, 2)).astype(ml_dtypes.float8_e4m3fn).view(np.uint8)
    return words, np.ascontiguousarray(byte.astype(np.uint8).reshape(k // 512, 16, n))


def unpack_weight(words, scales):
    g, p, n, _ = words.shape
    vals = np.ascontiguousarray(words).view(ml_dtypes.float8_e4m3fn).astype(np.float64) * np.repeat(np.exp2(scales.astype(np.float64) - 127.0), 8, axis=1)[..., None]
    return vals.transpose(0, 1, 3, 2).reshape(g * 512, n)


K, T, S, N, H = 1024, 2048, 512, 128, 512


def setup_inputs():
    n = np.random.standard_normal
    s = mx_kscale(K)[:, None]
    u = mx_kscale(H)
    packed_xT = pack_weight(n((K, T)) * s)
    return {
        "x_words": packed_xT[0],
        "x_scales": packed_xT[1],
        "w1": (n((K, H)) / np.sqrt(K) / s).astype(np.float32),
        "w2": (n((K, H)) / np.sqrt(K) / s).astype(np.float32),
        "dec": (np.random.uniform(0.2, 1.0, (H, S))).astype(np.float32),
        "inh": (np.random.uniform(0.2, 0.8, (H, S))).astype(np.float32),
        "unit": (np.random.uniform(0.6, 1.4, (H, 1)) * u[:, None]).astype(np.float32),
        "w3": (n((H, N)) / np.sqrt(H) / u[:, None]).astype(np.float32),
        "offs": striped(np.random.permutation(T)[:S]),
        "par": striped(np.random.permutation(S)),
        "sib": striped(np.random.permutation(S)),
    }


def reference(x_words, x_scales, w1, w2, dec, inh, unit, w3, offs, par, sib):
    xq = unpack_weight(x_words, x_scales)[:, unstriped(offs)]
    y = mxq(f64(w1), 0, "e4m3").T @ xq
    base = np.log(np.exp(y) + 1.0) + 0.2
    zz1 = mxq(f64(w2), 0, "e4m3").T @ xq
    exc = np.log(np.exp(zz1) + 1.0)
    ep = exc[:, unstriped(par)]
    trig = ep * f64(dec)
    zs = zz1[:, unstriped(sib)]
    inhb = zs * f64(inh)
    llam = np.log(np.exp(np.tanh(base + trig - inhb)) + 0.5)
    branch = trig / (base + trig + 0.1)
    hid = f64(unit) * (llam - (1.5 * branch))
    return mxq(f64(w3), 0, "e4m3").T @ mxq(hid, 0, "e4m3")

@@ -1,0 +1,260 @@
+from contextlib import ExitStack
+
+import concourse.mybir as mybir
+from concourse.masks import make_identity
+
+K, T, S, N, H = 1024, 2048, 512, 128, 512
+FLOPS = 2 * (2 * K * H * S + H * N * S)
+
+F32 = mybir.dt.float32
+BF16 = mybir.dt.bfloat16
+I32 = mybir.dt.int32
+U32 = mybir.dt.uint32
+U16 = mybir.dt.uint16
+U8 = mybir.dt.uint8
+FP8X4 = mybir.dt.float8_e4m3fn_x4
+ALU = mybir.AluOpType
+ACT = mybir.ActivationFunctionType
+
+P = 128
+PACK = 4
+K_PASS = P * PACK
+PASSES = K // K_PASS
+CHUNKS = S // P
+SPARE = 16
+LINEAR_FROM = 30.0
+
+
+def tile_picked_ylearnh_ll_p_kernel(
+    tc, x_words, x_scales, w1, w2, dec, inh, unit, w3, offs, par, sib, out
+):
+    nc = tc.nc
+    with ExitStack() as ctx:
+        keep = ctx.enter_context(tc.tile_pool(name="keep", bufs=1))
+        stage = ctx.enter_context(tc.tile_pool(name="stage", bufs=2))
+        psum = ctx.enter_context(tc.psum_pool(name="psum", bufs=1))
+
+        def sb(shape, dtype, name, tag=None):
+            return keep.tile(shape, dtype, name=name, tag=tag or name, align_bytes=64)
+
+        def bank(group, t, shape, name):
+            return psum.tile(shape, F32, name=name, tag="bank%s%d" % (group, t))
+
+        def load_weight(w, g, name):
+            raw = sb([P, PACK, H], F32, name)
+            nc.sync.dma_start(out=raw[:], in_=w[g * K_PASS : (g + 1) * K_PASS, :].rearrange("(p j) c -> p j c", j=PACK))
+            return raw
+
+        def load_rows(src, t, name):
+            rows = sb([P, S], F32, name)
+            nc.sync.dma_start(out=rows[:], in_=src.rearrange("(p t) s -> p t s", t=PACK)[:, t, :])
+            return rows
+
+        def load_list(src, name):
+            lst = sb([P, S // 16], U16, name)
+            nc.sync.dma_start(lst[:], src)
+            return lst
+
+        def quantise_weight(raw, name, tag=None):
+            grouped = stage.tile([P, PACK * H], BF16, name="grouped", align_bytes=64)
+            nc.vector.tensor_copy(
+                out=grouped[:].rearrange("p (t m j) -> p m j t", t=PACK, j=PACK),
+                in_=raw[:].rearrange("p j (m t) -> p m j t", t=PACK),
+            )
+            codes = sb([P, H], U32, name + "_codes", tag)
+            scales = sb([P, H], U8, name + "_scales")
+            nc.vector.quantize_mx(out=codes[:].bitcast(FP8X4), scales=scales[:], in_=grouped[:])
+            return codes, scales
+
+        def product(acc, weights, t):
+            cols = slice(t * P, (t + 1) * P)
+            for g in range(PASSES):
+                codes, scales = weights[g]
+                nc.tensor.matmul_mx(
+                    out=acc[:],
+                    lhsT=codes[:, cols].bitcast(FP8X4),
+                    lhsT_scale=scales[:, cols],
+                    rhs=x_codes[g][:].bitcast(FP8X4),
+                    rhs_scale=x_planes[4 * g : P, :],
+                    start=(g == 0),
+                    stop=(g == PASSES - 1),
+                )
+
+        def transposed_sum(acc, terms):
+            for a, term in enumerate(terms):
+                for b in range(PACK):
+                    nc.tensor.matmul(
+                        out=acc[:, b, :],
+                        lhsT=term(b),
+                        rhs=ident[:],
+                        is_transpose=True,
+                        start=(a == 0 and b == 0),
+                        stop=(a == len(terms) - 1 and b == PACK - 1),
+                    )
+
+        def blocks(tile):
+            return lambda b: tile[:, b * P : (b + 1) * P]
+
+        offs_sb = load_list(offs, "offs_sb")
+        table_scales = sb([P, T], U8, "table_scales")
+        nc.gpsimd.memset(table_scales[:].bitcast(I32), 0)
+        w2_raw = [load_weight(w2, 0, "w2_raw0")]
+        for q in range(4):
+            nc.sync.dma_start(
+                out=table_scales[32 * q : 32 * q + 8, :].bitcast(I32),
+                in_=x_scales[:, 4 * q : 4 * q + 4, :].bitcast(I32),
+            )
+        w2_raw.append(load_weight(w2, 1, "w2_raw1"))
+        table_words = []
+        for g in range(PASSES):
+            words = sb([P, T], U32, "table_words%d" % g)
+            nc.sync.dma_start(out=words[:].bitcast(I32), in_=x_words[g].rearrange("p c r -> p (c r)").bitcast(I32))
+            table_words.append(words)
+        w1_raw = [load_weight(w1, g, "w1_raw%d" % g) for g in range(PASSES)]
+        par_sb = load_list(par, "par_sb")
+        dec_sb = [load_rows(dec, t, "dec%d" % t) for t in range(PACK)]
+        sib_sb = load_list(sib, "sib_sb")
+        inh_sb = [load_rows(inh, t, "inh%d" % t) for t in range(PACK)]
+        unit_sb = sb([P, PACK], F32, "unit_sb")
+        nc.sync.dma_start(out=unit_sb[:], in_=unit.rearrange("(p t) o -> p (t o)", t=PACK))
+        w3_raw = sb([P, PACK, N], F32, "w3_raw")
+        nc.sync.dma_start(out=w3_raw[:], in_=w3.rearrange("(p j) n -> p j n", j=PACK))
+
+        ident = sb([P, P], F32, "ident")
+        make_identity(nc, ident[:])
+        neg_z = [sb([P, S + SPARE], F32, "neg_z%d" % t) for t in range(PACK)]
+        exc = [sb([P, S + SPARE], F32, "exc%d" % t) for t in range(PACK)]
+        for window in neg_z + exc:
+            nc.gpsimd.memset(window[:, S:], 0.0)
+
+        w2_q = [quantise_weight(w2_raw[0], "w2q0")]
+        x_planes = sb([P, S], U8, "x_planes")
+        nc.vector.tensor_copy(x_planes[:], table_scales[:].indirect(offs_sb[:]))
+        w2_q.append(quantise_weight(w2_raw[1], "w2q1"))
+        x_codes = []
+        for g in range(PASSES):
+            picked = sb([P, S], U32, "x_codes%d" % g)
+            nc.vector.tensor_copy(picked[:], table_words[g][:].indirect(offs_sb[:]))
+            x_codes.append(picked)
+
+        def softplus_logs(acc, name):
+            logs = sb([P, PACK, S], F32, name)
+            for t in range(PACK):
+                nc.scalar.activation(out=logs[:, t, :], in_=acc[t][:], func=ACT.Exp)
+            for t in range(PACK):
+                nc.scalar.activation(out=logs[:, t, :], in_=logs[:, t, :], func=ACT.Ln, bias=1.0)
+            return logs
+
+        def softplus(dst, logs, acc):
+            nc.vector.scalar_tensor_tensor(out=dst, in0=logs, scalar=LINEAR_FROM, in1=acc, op0=ALU.min, op1=ALU.max)
+
+        z_ps = []
+        for t in range(PACK):
+            acc = bank("a", t, [P, S], "z_ps%d" % t)
+            product(acc, w2_q, t)
+            z_ps.append(acc)
+        z_logs = softplus_logs(z_ps, "z_logs")
+
+        w1_q = [quantise_weight(w1_raw[g], "w1q%d" % g) for g in range(PASSES)]
+        y_ps = []
+        for t in range(PACK):
+            acc = bank("b", t, [P, S], "y_ps%d" % t)
+            product(acc, w1_q, t)
+            y_ps.append(acc)
+        y_logs = softplus_logs(y_ps, "y_logs")
+
+        trig, soft_y, neg_inhb = [], [], []
+        for t in range(PACK):
+            softplus(exc[t][:, :S], z_logs[:, t, :], z_ps[t][:])
+        for t in range(PACK):
+            prod = sb([P, S], F32, "trig%d" % t)
+            nc.vector.tensor_tensor(prod[:], exc[t][:].indirect(par_sb[:]), dec_sb[t][:], ALU.mult)
+            trig.append(prod)
+        log_den = sb([P, PACK, S], F32, "log_den", "after_den")
+        for t in range(PACK):
+            soft = sb([P, S], F32, "soft_y%d" % t)
+            softplus(soft[:], y_logs[:, t, :], y_ps[t][:])
+            soft_y.append(soft)
+            den_ps = bank("b", t, [P, CHUNKS, P], "den_ps%d" % t)
+            transposed_sum(den_ps, [blocks(trig[t]), blocks(soft_y[t])])
+            nc.scalar.activation(
+                out=log_den[:, t, :], in_=den_ps[:].rearrange("p c m -> p (c m)"), func=ACT.Ln, bias=0.3
+            )
+        for t in range(PACK):
+            nc.vector.tensor_scalar_mul(neg_z[t][:, :S], z_ps[t][:], -1.0)
+        for t in range(PACK):
+            prod = sb([P, S], F32, "neg_inhb%d" % t)
+            nc.vector.tensor_tensor(prod[:], neg_z[t][:].indirect(sib_sb[:]), inh_sb[t][:], ALU.mult)
+            neg_inhb.append(prod)
+
+        w3_grouped = sb([P, PACK * N], BF16, "w3_grouped")
+        nc.vector.tensor_copy(
+            out=w3_grouped[:].rearrange("p (c i j) -> p c j i", i=4, j=PACK),
+            in_=w3_raw[:].rearrange("p j (c i) -> p c j i", i=4),
+        )
+        w3_codes = sb([P, N], U32, "w3_codes")
+        w3_scales = sb([P, N], U8, "w3_scales")
+        nc.vector.quantize_mx(out=w3_codes[:].bitcast(FP8X4), scales=w3_scales[:], in_=w3_grouped[:])
+
+        u_ps, trig_ps = [], []
+        for t in range(PACK):
+            acc = bank("a", t, [P, CHUNKS, P], "u_ps%d" % t)
+            transposed_sum(acc, [blocks(trig[t]), blocks(soft_y[t]), blocks(neg_inhb[t])])
+            u_ps.append(acc)
+        for t in range(PACK):
+            acc = bank("b", t, [P, CHUNKS, P], "trig_ps%d" % t)
+            transposed_sum(acc, [blocks(trig[t])])
+            trig_ps.append(acc)
+
+        rec = sb([P, PACK, S], F32, "rec")
+        nc.scalar.activation(out=rec[:], in_=log_den[:], func=ACT.Exp, scale=-1.0)
+        bounded = sb([P, PACK, CHUNKS, P], F32, "bounded", "after_den")
+        for t in range(PACK):
+            nc.scalar.activation(out=bounded[:, t, :, :], in_=u_ps[t][:], func=ACT.Tanh, bias=0.2)
+        bounded_flat = bounded[:].rearrange("p t c m -> p (t c m)")
+        nc.scalar.activation(out=bounded_flat, in_=bounded_flat, func=ACT.Exp)
+
+        share = []
+        for t in range(PACK):
+            prod = sb([P, S], F32, "share%d" % t)
+            nc.vector.scalar_tensor_tensor(
+                out=prod[:],
+                in0=trig_ps[t][:].rearrange("p c m -> p (c m)"),
+                scalar=-1.5,
+                in1=rec[:, t, :],
+                op0=ALU.mult,
+                op1=ALU.mult,
+            )
+            share.append(prod)
+
+        for c in range(CHUNKS):
+            cols = slice(c * P, (c + 1) * P)
+            llam = sb([P, PACK, P], F32, "llam%d" % c)
+            nc.scalar.activation(out=llam[:], in_=bounded[:, :, c, :], func=ACT.Ln, bias=0.5)
+            hid_ps = bank("a", c, [P, PACK, P], "hid_ps%d" % c)
+            transposed_sum(hid_ps, [lambda t: share[t][:, cols], lambda t: llam[:, t, :]])
+            hid = sb([P, P, PACK], BF16, "hid%d" % c)
+            nc.vector.tensor_tensor(
+                out=hid[:],
+                in0=hid_ps[:].rearrange("p t j -> p j t"),
+                in1=unit_sb[:].unsqueeze(1).to_broadcast([P, P, PACK]),
+                op=ALU.mult,
+            )
+            hid_codes = sb([P, P], U32, "hid_codes%d" % c)
+            hid_scales = sb([P, P], U8, "hid_scales%d" % c)
+            nc.vector.quantize_mx(
+                out=hid_codes[:].bitcast(FP8X4), scales=hid_scales[:], in_=hid[:].rearrange("p j t -> p (j t)")
+            )
+            out_ps = bank("b", c, [P, P], "out_ps%d" % c)
+            nc.tensor.matmul_mx(
+                out=out_ps[:],
+                lhsT=w3_codes[:].bitcast(FP8X4),
+                lhsT_scale=w3_scales[:],
+                rhs=hid_codes[:].bitcast(FP8X4),
+                rhs_scale=hid_scales[:],
+                start=True,
+                stop=True,
+            )
+            result = sb([P, P], F32, "result%d" % c)
+            nc.scalar.copy(out=result[:], in_=out_ps[:])
+            nc.sync.dma_start(out=out[:, cols], in_=result[:])

@@ -40,14 +40,15 @@ def tile_picked_ylearnh_ll_p_kernel(
         def bank(group, t, shape, name):
             return psum.tile(shape, F32, name=name, tag="bank%s%d" % (group, t))
 
-        def load_weight(w, g, name):
-            raw = sb([P, PACK, H], F32, name)
-            nc.sync.dma_start(out=raw[:], in_=w[g * K_PASS : (g + 1) * K_PASS, :].rearrange("(p j) c -> p j c", j=PACK))
+        def load_weight(w, g, cols, name):
+            raw = sb([P, PACK, cols.stop - cols.start], F32, name)
+            rows = w[g * K_PASS : (g + 1) * K_PASS, cols]
+            nc.sync.dma_start(out=raw[:], in_=rows.rearrange("(p j) c -> p j c", j=PACK))
             return raw
 
-        def load_rows(src, t, name):
+        def load_rows(src, a, name):
             rows = sb([P, S], F32, name)
-            nc.sync.dma_start(out=rows[:], in_=src.rearrange("(p t) s -> p t s", t=PACK)[:, t, :])
+            nc.sync.dma_start(out=rows[:], in_=src[a * P : (a + 1) * P, :])
             return rows
 
         def load_list(src, name):
@@ -56,29 +57,32 @@ def tile_picked_ylearnh_ll_p_kernel(
             return lst
 
         def quantise_weight(raw, name, tag=None):
-            grouped = stage.tile([P, PACK * H], BF16, name="grouped", align_bytes=64)
+            width = raw.shape[2]
+            grouped = stage.tile([P, PACK * width], BF16, name="grouped", align_bytes=64)
             nc.vector.tensor_copy(
-                out=grouped[:].rearrange("p (t m j) -> p m j t", t=PACK, j=PACK),
-                in_=raw[:].rearrange("p j (m t) -> p m j t", t=PACK),
+                out=grouped[:].rearrange("p (c i j) -> p c j i", i=4, j=PACK),
+                in_=raw[:].rearrange("p j (c i) -> p c j i", i=4),
             )
-            codes = sb([P, H], U32, name + "_codes", tag)
-            scales = sb([P, H], U8, name + "_scales")
+            codes = sb([P, width], U32, name + "_codes", tag)
+            scales = sb([P, width], U8, name + "_scales")
             nc.vector.quantize_mx(out=codes[:].bitcast(FP8X4), scales=scales[:], in_=grouped[:])
-            return codes, scales
+            return [(codes[:, c : c + P], scales[:, c : c + P]) for c in range(0, width, P)]
 
-        def product(acc, weights, t):
-            cols = slice(t * P, (t + 1) * P)
+        def product(acc, weights, a):
             for g in range(PASSES):
-                codes, scales = weights[g]
+                codes, scales = weights[g][a]
                 nc.tensor.matmul_mx(
                     out=acc[:],
-                    lhsT=codes[:, cols].bitcast(FP8X4),
-                    lhsT_scale=scales[:, cols],
+                    lhsT=codes.bitcast(FP8X4),
+                    lhsT_scale=scales,
                     rhs=x_codes[g][:].bitcast(FP8X4),
                     rhs_scale=x_planes[4 * g : P, :],
                     start=(g == 0),
                     stop=(g == PASSES - 1),
                 )
+
+        def dealt(acc):
+            return acc[:].rearrange("p c (m t) -> p t c m", t=PACK)
 
         def transposed_sum(acc, terms):
             for a, term in enumerate(terms):
@@ -96,21 +100,19 @@ def tile_picked_ylearnh_ll_p_kernel(
             return lambda b: tile[:, b * P : (b + 1) * P]
 
         offs_sb = load_list(offs, "offs_sb")
-        table_scales = sb([P, T], U8, "table_scales")
-        nc.gpsimd.memset(table_scales[:].bitcast(I32), 0)
-        w2_raw = [load_weight(w2, 0, "w2_raw0")]
+        scale_rows = sb([P, T // 4], I32, "scale_rows")
         for q in range(4):
             nc.sync.dma_start(
-                out=table_scales[32 * q : 32 * q + 8, :].bitcast(I32),
-                in_=x_scales[:, 4 * q : 4 * q + 4, :].bitcast(I32),
+                out=scale_rows[32 * q : 32 * q + 8, :], in_=x_scales[:, 4 * q : 4 * q + 4, :].bitcast(I32)
             )
-        w2_raw.append(load_weight(w2, 1, "w2_raw1"))
+        w2_first = load_weight(w2, 0, slice(0, H), "w2_first")
         table_words = []
         for g in range(PASSES):
             words = sb([P, T], U32, "table_words%d" % g)
             nc.sync.dma_start(out=words[:].bitcast(I32), in_=x_words[g].rearrange("p c r -> p (c r)").bitcast(I32))
             table_words.append(words)
-        w1_raw = [load_weight(w1, g, "w1_raw%d" % g) for g in range(PASSES)]
+        w2_last = [load_weight(w2, 1, slice(c, c + H // 2), "w2_last%d" % c) for c in (0, H // 2)]
+        w1_raw = [load_weight(w1, g, slice(0, H), "w1_raw%d" % g) for g in range(PASSES)]
         par_sb = load_list(par, "par_sb")
         dec_sb = [load_rows(dec, t, "dec%d" % t) for t in range(PACK)]
         sib_sb = load_list(sib, "sib_sb")
@@ -127,22 +129,29 @@ def tile_picked_ylearnh_ll_p_kernel(
         for window in neg_z + exc:
             nc.gpsimd.memset(window[:, S:], 0.0)
 
-        w2_q = [quantise_weight(w2_raw[0], "w2q0")]
+        table_scales = sb([P, T], U8, "table_scales")
+        nc.vector.memset(table_scales[:].bitcast(I32), 0)
+        for q in range(4):
+            rows = slice(32 * q, 32 * q + 8)
+            nc.vector.tensor_copy(table_scales[rows, :].bitcast(I32), scale_rows[rows, :])
         x_planes = sb([P, S], U8, "x_planes")
         nc.vector.tensor_copy(x_planes[:], table_scales[:].indirect(offs_sb[:]))
-        w2_q.append(quantise_weight(w2_raw[1], "w2q1"))
+        w2_q = [quantise_weight(w2_first, "w2q0")]
         x_codes = []
         for g in range(PASSES):
             picked = sb([P, S], U32, "x_codes%d" % g)
             nc.vector.tensor_copy(picked[:], table_words[g][:].indirect(offs_sb[:]))
             x_codes.append(picked)
 
-        def softplus_logs(acc, name):
-            logs = sb([P, PACK, S], F32, name)
+        w2_q.append(quantise_weight(w2_last[0], "w2q1") + quantise_weight(w2_last[1], "w2q2", "after_z"))
+
+        def softplus_logs(acc, name, tag):
+            exps = sb([P, PACK, S], F32, name + "_exps", "exps")
             for t in range(PACK):
-                nc.scalar.activation(out=logs[:, t, :], in_=acc[t][:], func=ACT.Exp)
+                nc.scalar.activation(out=exps[:, t, :], in_=acc[t][:], func=ACT.Exp)
+            logs = sb([P, PACK, S], F32, name, tag)
             for t in range(PACK):
-                nc.scalar.activation(out=logs[:, t, :], in_=logs[:, t, :], func=ACT.Ln, bias=1.0)
+                nc.scalar.activation(out=logs[:, t, :], in_=exps[:, t, :], func=ACT.Ln, bias=1.0)
             return logs
 
         def softplus(dst, logs, acc):
@@ -153,7 +162,7 @@ def tile_picked_ylearnh_ll_p_kernel(
             acc = bank("a", t, [P, S], "z_ps%d" % t)
             product(acc, w2_q, t)
             z_ps.append(acc)
-        z_logs = softplus_logs(z_ps, "z_logs")
+        z_logs = softplus_logs(z_ps, "z_logs", "after_z")
 
         w1_q = [quantise_weight(w1_raw[g], "w1q%d" % g) for g in range(PASSES)]
         y_ps = []
@@ -161,78 +170,73 @@ def tile_picked_ylearnh_ll_p_kernel(
             acc = bank("b", t, [P, S], "y_ps%d" % t)
             product(acc, w1_q, t)
             y_ps.append(acc)
-        y_logs = softplus_logs(y_ps, "y_logs")
+        y_logs = softplus_logs(y_ps, "y_logs", "y_logs")
 
         trig, soft_y, neg_inhb = [], [], []
+        for t in range(PACK):
+            nc.vector.tensor_scalar_mul(neg_z[t][:, :S], z_ps[t][:], -1.0)
         for t in range(PACK):
             softplus(exc[t][:, :S], z_logs[:, t, :], z_ps[t][:])
         for t in range(PACK):
             prod = sb([P, S], F32, "trig%d" % t)
             nc.vector.tensor_tensor(prod[:], exc[t][:].indirect(par_sb[:]), dec_sb[t][:], ALU.mult)
             trig.append(prod)
-        log_den = sb([P, PACK, S], F32, "log_den", "after_den")
+        log_den = sb([P, PACK, CHUNKS, PACK, P // PACK], F32, "log_den", "after_den")
         for t in range(PACK):
             soft = sb([P, S], F32, "soft_y%d" % t)
             softplus(soft[:], y_logs[:, t, :], y_ps[t][:])
             soft_y.append(soft)
-            den_ps = bank("b", t, [P, CHUNKS, P], "den_ps%d" % t)
+            den_ps = bank("a", t, [P, CHUNKS, P], "den_ps%d" % t)
             transposed_sum(den_ps, [blocks(trig[t]), blocks(soft_y[t])])
-            nc.scalar.activation(
-                out=log_den[:, t, :], in_=den_ps[:].rearrange("p c m -> p (c m)"), func=ACT.Ln, bias=0.3
-            )
-        for t in range(PACK):
-            nc.vector.tensor_scalar_mul(neg_z[t][:, :S], z_ps[t][:], -1.0)
+            nc.scalar.activation(out=log_den[:, :, :, t, :], in_=dealt(den_ps), func=ACT.Ln, bias=0.3)
         for t in range(PACK):
             prod = sb([P, S], F32, "neg_inhb%d" % t)
             nc.vector.tensor_tensor(prod[:], neg_z[t][:].indirect(sib_sb[:]), inh_sb[t][:], ALU.mult)
             neg_inhb.append(prod)
 
-        w3_grouped = sb([P, PACK * N], BF16, "w3_grouped")
-        nc.vector.tensor_copy(
-            out=w3_grouped[:].rearrange("p (c i j) -> p c j i", i=4, j=PACK),
-            in_=w3_raw[:].rearrange("p j (c i) -> p c j i", i=4),
-        )
-        w3_codes = sb([P, N], U32, "w3_codes")
-        w3_scales = sb([P, N], U8, "w3_scales")
-        nc.vector.quantize_mx(out=w3_codes[:].bitcast(FP8X4), scales=w3_scales[:], in_=w3_grouped[:])
+        ((w3_codes, w3_scales),) = quantise_weight(w3_raw, "w3q")
 
         u_ps, trig_ps = [], []
         for t in range(PACK):
-            acc = bank("a", t, [P, CHUNKS, P], "u_ps%d" % t)
+            acc = bank("b", t, [P, CHUNKS, P], "u_ps%d" % t)
             transposed_sum(acc, [blocks(trig[t]), blocks(soft_y[t]), blocks(neg_inhb[t])])
             u_ps.append(acc)
         for t in range(PACK):
-            acc = bank("b", t, [P, CHUNKS, P], "trig_ps%d" % t)
+            acc = bank("a", t, [P, CHUNKS, P], "trig_ps%d" % t)
             transposed_sum(acc, [blocks(trig[t])])
             trig_ps.append(acc)
 
-        rec = sb([P, PACK, S], F32, "rec")
-        nc.scalar.activation(out=rec[:], in_=log_den[:], func=ACT.Exp, scale=-1.0)
-        bounded = sb([P, PACK, CHUNKS, P], F32, "bounded", "after_den")
+        flat = "p t c a m -> p (t c a m)"
+        rec = sb([P, PACK, CHUNKS, PACK, P // PACK], F32, "rec")
+        nc.scalar.activation(out=rec[:].rearrange(flat), in_=log_den[:].rearrange(flat), func=ACT.Exp, scale=-1.0)
+        bounded = sb([P, PACK, CHUNKS, PACK, P // PACK], F32, "bounded", "after_den")
         for t in range(PACK):
-            nc.scalar.activation(out=bounded[:, t, :, :], in_=u_ps[t][:], func=ACT.Tanh, bias=0.2)
-        bounded_flat = bounded[:].rearrange("p t c m -> p (t c m)")
-        nc.scalar.activation(out=bounded_flat, in_=bounded_flat, func=ACT.Exp)
+            nc.scalar.activation(out=bounded[:, :, :, t, :], in_=dealt(u_ps[t]), func=ACT.Tanh, bias=0.2)
+        nc.scalar.activation(out=bounded[:].rearrange(flat), in_=bounded[:].rearrange(flat), func=ACT.Exp)
 
-        share = []
+        share = sb([P, PACK, CHUNKS, PACK, P // PACK], F32, "share")
         for t in range(PACK):
-            prod = sb([P, S], F32, "share%d" % t)
             nc.vector.scalar_tensor_tensor(
-                out=prod[:],
-                in0=trig_ps[t][:].rearrange("p c m -> p (c m)"),
+                out=share[:, :, :, t, :],
+                in0=dealt(trig_ps[t]),
                 scalar=-1.5,
-                in1=rec[:, t, :],
+                in1=rec[:, :, :, t, :],
                 op0=ALU.mult,
                 op1=ALU.mult,
             )
-            share.append(prod)
 
         for c in range(CHUNKS):
             cols = slice(c * P, (c + 1) * P)
             llam = sb([P, PACK, P], F32, "llam%d" % c)
-            nc.scalar.activation(out=llam[:], in_=bounded[:, :, c, :], func=ACT.Ln, bias=0.5)
-            hid_ps = bank("a", c, [P, PACK, P], "hid_ps%d" % c)
-            transposed_sum(hid_ps, [lambda t: share[t][:, cols], lambda t: llam[:, t, :]])
+            for slots in (slice(0, PACK // 2), slice(PACK // 2, PACK)):
+                nc.scalar.activation(
+                    out=llam[:, slots, :],
+                    in_=bounded[:, slots, c, :, :].rearrange("p t a m -> p t (a m)"),
+                    func=ACT.Ln,
+                    bias=0.5,
+                )
+            hid_ps = bank("b", c, [P, PACK, P], "hid_ps%d" % c)
+            transposed_sum(hid_ps, [lambda t: share[:, t, c, :, :].rearrange("p a m -> p (a m)"), lambda t: llam[:, t, :]])
             hid = sb([P, P, PACK], BF16, "hid%d" % c)
             nc.vector.tensor_tensor(
                 out=hid[:],
@@ -245,11 +249,11 @@ def tile_picked_ylearnh_ll_p_kernel(
             nc.vector.quantize_mx(
                 out=hid_codes[:].bitcast(FP8X4), scales=hid_scales[:], in_=hid[:].rearrange("p j t -> p (j t)")
             )
-            out_ps = bank("b", c, [P, P], "out_ps%d" % c)
+            out_ps = bank("a", c, [P, P], "out_ps%d" % c)
             nc.tensor.matmul_mx(
                 out=out_ps[:],
-                lhsT=w3_codes[:].bitcast(FP8X4),
-                lhsT_scale=w3_scales[:],
+                lhsT=w3_codes.bitcast(FP8X4),
+                lhsT_scale=w3_scales,
                 rhs=hid_codes[:].bitcast(FP8X4),
                 rhs_scale=hid_scales[:],
                 start=True,

from contextlib import ExitStack

import concourse.mybir as mybir
from concourse.masks import make_identity

K, T, S, N, H = 1024, 2048, 512, 128, 512
FLOPS = 2 * (2 * K * H * S + H * N * S)

F32 = mybir.dt.float32
BF16 = mybir.dt.bfloat16
I32 = mybir.dt.int32
U32 = mybir.dt.uint32
U16 = mybir.dt.uint16
U8 = mybir.dt.uint8
FP8X4 = mybir.dt.float8_e4m3fn_x4
ALU = mybir.AluOpType
ACT = mybir.ActivationFunctionType

P = 128
PACK = 4
K_PASS = P * PACK
PASSES = K // K_PASS
CHUNKS = S // P
SPARE = 16
LINEAR_FROM = 30.0


def tile_picked_ylearnh_ll_p_kernel(
    tc, x_words, x_scales, w1, w2, dec, inh, unit, w3, offs, par, sib, out
):
    nc = tc.nc
    with ExitStack() as ctx:
        keep = ctx.enter_context(tc.tile_pool(name="keep", bufs=1))
        stage = ctx.enter_context(tc.tile_pool(name="stage", bufs=2))
        psum = ctx.enter_context(tc.psum_pool(name="psum", bufs=1))

        def sb(shape, dtype, name, tag=None):
            return keep.tile(shape, dtype, name=name, tag=tag or name, align_bytes=64)

        def bank(group, t, shape, name):
            return psum.tile(shape, F32, name=name, tag="bank%s%d" % (group, t))

        def load_weight(w, g, cols, name):
            raw = sb([P, PACK, cols.stop - cols.start], F32, name)
            rows = w[g * K_PASS : (g + 1) * K_PASS, cols]
            nc.sync.dma_start(out=raw[:], in_=rows.rearrange("(p j) c -> p j c", j=PACK))
            return raw

        def load_rows(src, a, name):
            rows = sb([P, S], F32, name)
            nc.sync.dma_start(out=rows[:], in_=src[a * P : (a + 1) * P, :])
            return rows

        def load_list(src, name):
            lst = sb([P, S // 16], U16, name)
            nc.sync.dma_start(lst[:], src)
            return lst

        def quantise_weight(raw, name, tag=None):
            width = raw.shape[2]
            grouped = stage.tile([P, PACK * width], BF16, name="grouped", align_bytes=64)
            nc.vector.tensor_copy(
                out=grouped[:].rearrange("p (c i j) -> p c j i", i=4, j=PACK),
                in_=raw[:].rearrange("p j (c i) -> p c j i", i=4),
            )
            codes = sb([P, width], U32, name + "_codes", tag)
            scales = sb([P, width], U8, name + "_scales")
            nc.vector.quantize_mx(out=codes[:].bitcast(FP8X4), scales=scales[:], in_=grouped[:])
            return [(codes[:, c : c + P], scales[:, c : c + P]) for c in range(0, width, P)]

        def product(acc, weights, a):
            for g in range(PASSES):
                codes, scales = weights[g][a]
                nc.tensor.matmul_mx(
                    out=acc[:],
                    lhsT=codes.bitcast(FP8X4),
                    lhsT_scale=scales,
                    rhs=x_codes[g][:].bitcast(FP8X4),
                    rhs_scale=x_planes[4 * g : P, :],
                    start=(g == 0),
                    stop=(g == PASSES - 1),
                )

        def dealt(acc):
            return acc[:].rearrange("p c (m t) -> p t c m", t=PACK)

        def transposed_sum(acc, terms):
            for a, term in enumerate(terms):
                for b in range(PACK):
                    nc.tensor.matmul(
                        out=acc[:, b, :],
                        lhsT=term(b),
                        rhs=ident[:],
                        is_transpose=True,
                        start=(a == 0 and b == 0),
                        stop=(a == len(terms) - 1 and b == PACK - 1),
                    )

        def blocks(tile):
            return lambda b: tile[:, b * P : (b + 1) * P]

        offs_sb = load_list(offs, "offs_sb")
        scale_rows = sb([P, T // 4], I32, "scale_rows")
        for q in range(4):
            nc.sync.dma_start(
                out=scale_rows[32 * q : 32 * q + 8, :], in_=x_scales[:, 4 * q : 4 * q + 4, :].bitcast(I32)
            )
        w2_first = load_weight(w2, 0, slice(0, H), "w2_first")
        table_words = []
        for g in range(PASSES):
            words = sb([P, T], U32, "table_words%d" % g)
            nc.sync.dma_start(out=words[:].bitcast(I32), in_=x_words[g].rearrange("p c r -> p (c r)").bitcast(I32))
            table_words.append(words)
        w2_last = [load_weight(w2, 1, slice(c, c + H // 2), "w2_last%d" % c) for c in (0, H // 2)]
        w1_raw = [load_weight(w1, g, slice(0, H), "w1_raw%d" % g) for g in range(PASSES)]
        par_sb = load_list(par, "par_sb")
        dec_sb = [load_rows(dec, t, "dec%d" % t) for t in range(PACK)]
        sib_sb = load_list(sib, "sib_sb")
        inh_sb = [load_rows(inh, t, "inh%d" % t) for t in range(PACK)]
        unit_sb = sb([P, PACK], F32, "unit_sb")
        nc.sync.dma_start(out=unit_sb[:], in_=unit.rearrange("(p t) o -> p (t o)", t=PACK))
        w3_raw = sb([P, PACK, N], F32, "w3_raw")
        nc.sync.dma_start(out=w3_raw[:], in_=w3.rearrange("(p j) n -> p j n", j=PACK))

        ident = sb([P, P], F32, "ident")
        make_identity(nc, ident[:])
        neg_z = [sb([P, S + SPARE], F32, "neg_z%d" % t) for t in range(PACK)]
        exc = [sb([P, S + SPARE], F32, "exc%d" % t) for t in range(PACK)]
        for window in neg_z + exc:
            nc.gpsimd.memset(window[:, S:], 0.0)

        table_scales = sb([P, T], U8, "table_scales")
        nc.vector.memset(table_scales[:].bitcast(I32), 0)
        for q in range(4):
            rows = slice(32 * q, 32 * q + 8)
            nc.vector.tensor_copy(table_scales[rows, :].bitcast(I32), scale_rows[rows, :])
        x_planes = sb([P, S], U8, "x_planes")
        nc.vector.tensor_copy(x_planes[:], table_scales[:].indirect(offs_sb[:]))
        w2_q = [quantise_weight(w2_first, "w2q0")]
        x_codes = []
        for g in range(PASSES):
            picked = sb([P, S], U32, "x_codes%d" % g)
            nc.vector.tensor_copy(picked[:], table_words[g][:].indirect(offs_sb[:]))
            x_codes.append(picked)

        w2_q.append(quantise_weight(w2_last[0], "w2q1") + quantise_weight(w2_last[1], "w2q2", "after_z"))

        def softplus_logs(acc, name, tag):
            exps = sb([P, PACK, S], F32, name + "_exps", "exps")
            for t in range(PACK):
                nc.scalar.activation(out=exps[:, t, :], in_=acc[t][:], func=ACT.Exp)
            logs = sb([P, PACK, S], F32, name, tag)
            for t in range(PACK):
                nc.scalar.activation(out=logs[:, t, :], in_=exps[:, t, :], func=ACT.Ln, bias=1.0)
            return logs

        def softplus(dst, logs, acc):
            nc.vector.scalar_tensor_tensor(out=dst, in0=logs, scalar=LINEAR_FROM, in1=acc, op0=ALU.min, op1=ALU.max)

        z_ps = []
        for t in range(PACK):
            acc = bank("a", t, [P, S], "z_ps%d" % t)
            product(acc, w2_q, t)
            z_ps.append(acc)
        z_logs = softplus_logs(z_ps, "z_logs", "after_z")

        w1_q = [quantise_weight(w1_raw[g], "w1q%d" % g) for g in range(PASSES)]
        y_ps = []
        for t in range(PACK):
            acc = bank("b", t, [P, S], "y_ps%d" % t)
            product(acc, w1_q, t)
            y_ps.append(acc)
        y_logs = softplus_logs(y_ps, "y_logs", "y_logs")

        trig, soft_y, neg_inhb = [], [], []
        for t in range(PACK):
            nc.vector.tensor_scalar_mul(neg_z[t][:, :S], z_ps[t][:], -1.0)
        for t in range(PACK):
            softplus(exc[t][:, :S], z_logs[:, t, :], z_ps[t][:])
        for t in range(PACK):
            prod = sb([P, S], F32, "trig%d" % t)
            nc.vector.tensor_tensor(prod[:], exc[t][:].indirect(par_sb[:]), dec_sb[t][:], ALU.mult)
            trig.append(prod)
        log_den = sb([P, PACK, CHUNKS, PACK, P // PACK], F32, "log_den", "after_den")
        for t in range(PACK):
            soft = sb([P, S], F32, "soft_y%d" % t)
            softplus(soft[:], y_logs[:, t, :], y_ps[t][:])
            soft_y.append(soft)
            den_ps = bank("a", t, [P, CHUNKS, P], "den_ps%d" % t)
            transposed_sum(den_ps, [blocks(trig[t]), blocks(soft_y[t])])
            nc.scalar.activation(out=log_den[:, :, :, t, :], in_=dealt(den_ps), func=ACT.Ln, bias=0.3)
        for t in range(PACK):
            prod = sb([P, S], F32, "neg_inhb%d" % t)
            nc.vector.tensor_tensor(prod[:], neg_z[t][:].indirect(sib_sb[:]), inh_sb[t][:], ALU.mult)
            neg_inhb.append(prod)

        ((w3_codes, w3_scales),) = quantise_weight(w3_raw, "w3q")

        u_ps, trig_ps = [], []
        for t in range(PACK):
            acc = bank("b", t, [P, CHUNKS, P], "u_ps%d" % t)
            transposed_sum(acc, [blocks(trig[t]), blocks(soft_y[t]), blocks(neg_inhb[t])])
            u_ps.append(acc)
        for t in range(PACK):
            acc = bank("a", t, [P, CHUNKS, P], "trig_ps%d" % t)
            transposed_sum(acc, [blocks(trig[t])])
            trig_ps.append(acc)

        flat = "p t c a m -> p (t c a m)"
        rec = sb([P, PACK, CHUNKS, PACK, P // PACK], F32, "rec")
        nc.scalar.activation(out=rec[:].rearrange(flat), in_=log_den[:].rearrange(flat), func=ACT.Exp, scale=-1.0)
        bounded = sb([P, PACK, CHUNKS, PACK, P // PACK], F32, "bounded", "after_den")
        for t in range(PACK):
            nc.scalar.activation(out=bounded[:, :, :, t, :], in_=dealt(u_ps[t]), func=ACT.Tanh, bias=0.2)
        nc.scalar.activation(out=bounded[:].rearrange(flat), in_=bounded[:].rearrange(flat), func=ACT.Exp)

        share = sb([P, PACK, CHUNKS, PACK, P // PACK], F32, "share")
        for t in range(PACK):
            nc.vector.scalar_tensor_tensor(
                out=share[:, :, :, t, :],
                in0=dealt(trig_ps[t]),
                scalar=-1.5,
                in1=rec[:, :, :, t, :],
                op0=ALU.mult,
                op1=ALU.mult,
            )

        for c in range(CHUNKS):
            cols = slice(c * P, (c + 1) * P)
            llam = sb([P, PACK, P], F32, "llam%d" % c)
            for slots in (slice(0, PACK // 2), slice(PACK // 2, PACK)):
                nc.scalar.activation(
                    out=llam[:, slots, :],
                    in_=bounded[:, slots, c, :, :].rearrange("p t a m -> p t (a m)"),
                    func=ACT.Ln,
                    bias=0.5,
                )
            hid_ps = bank("b", c, [P, PACK, P], "hid_ps%d" % c)
            transposed_sum(hid_ps, [lambda t: share[:, t, c, :, :].rearrange("p a m -> p (a m)"), lambda t: llam[:, t, :]])
            hid = sb([P, P, PACK], BF16, "hid%d" % c)
            nc.vector.tensor_tensor(
                out=hid[:],
                in0=hid_ps[:].rearrange("p t j -> p j t"),
                in1=unit_sb[:].unsqueeze(1).to_broadcast([P, P, PACK]),
                op=ALU.mult,
            )
            hid_codes = sb([P, P], U32, "hid_codes%d" % c)
            hid_scales = sb([P, P], U8, "hid_scales%d" % c)
            nc.vector.quantize_mx(
                out=hid_codes[:].bitcast(FP8X4), scales=hid_scales[:], in_=hid[:].rearrange("p j t -> p (j t)")
            )
            out_ps = bank("a", c, [P, P], "out_ps%d" % c)
            nc.tensor.matmul_mx(
                out=out_ps[:],
                lhsT=w3_codes.bitcast(FP8X4),
                lhsT_scale=w3_scales,
                rhs=hid_codes[:].bitcast(FP8X4),
                rhs_scale=hid_scales[:],
                start=True,
                stop=True,
            )
            result = sb([P, P], F32, "result%d" % c)
            nc.scalar.copy(out=result[:], in_=out_ps[:])
            nc.sync.dma_start(out=out[:, cols], in_=result[:])
